import numpy as np
import ml_dtypes


def mxq(x, axis, fmt="e4m3"):
    dtype, down = {"e4m3": (ml_dtypes.float8_e4m3fn, 7), "e5m2": (ml_dtypes.float8_e5m2, 14)}[fmt]
    v = np.moveaxis(np.asarray(x, np.float32).astype(ml_dtypes.bfloat16).astype(np.float64), axis, -1)
    blocks = v.reshape(v.shape[:-1] + (-1, 32))
    amax = np.abs(blocks).max(-1, keepdims=True)
    byte = np.maximum(np.where(amax > 0, np.frexp(amax)[1] - 1 + 127, 0) - down, 1)
    scale = np.exp2(byte - 127.0)
    codes = (blocks / scale).astype(np.float32).astype(dtype).astype(np.float64)
    return np.moveaxis((codes * scale).reshape(v.shape), -1, axis)


WIDE = False


def mx_kscale(k):
    if not WIDE:
        return np.ones(k)
    levels = np.array([10, -10, 5, -5, 0])
    if k % 512:
        return np.exp2(np.random.permutation(np.resize(levels, k // 32))).repeat(32)
    a = np.empty((k // 512, 16))
    for p in range(k // 512):
        a[p, :8] = np.random.permutation(np.resize(levels, 8))
        for g in range(8):
            far = levels[np.abs(levels - a[p, g]) >= 10]
            a[p, g + 8] = far[np.random.randint(len(far))]
    return np.exp2(a.ravel()).repeat(32)


def f64(x):
    return np.asarray(x).astype(np.float64)


def striped(idx):
    return np.tile(idx.reshape(-1, 16).T, (8, 1)).astype(np.uint16)


def unstriped(offs):
    return offs[:16].T.reshape(-1).astype(np.int64)


E2M1 = np.array([0.0, 0.5, 1.0, 1.5, 2.0, 3.0, 4.0, 6.0, -0.0, -0.5, -1.0, -1.5, -2.0, -3.0, -4.0, -6.0])


def pack_weight(w, fmt):
    k, n = w.shape
    w = f64(np.asarray(w, np.float32).astype(ml_dtypes.bfloat16)).reshape(k // 32, 32, n)
    amax = np.abs(w).max(1)
    if fmt == "e4m3":
        byte = np.frexp(amax)[1] - 1 + 127 - 7
    else:
        mant, ex = np.frexp(amax / 6.0)
        byte = np.where(mant > 0.5, ex, ex - 1) + 127
    byte = np.clip(np.where(amax > 0, byte, 1), 1, 254)
    scaled = (w * np.exp2(127.0 - byte)[:, None, :]).reshape(k, n).astype(np.float32)
    by_word = np.ascontiguousarray(scaled.reshape(k // 512, 128, 4, n).transpose(0, 1, 3, 2))
    if fmt == "e4m3":
        words = by_word.astype(ml_dtypes.float8_e4m3fn).view(np.uint8)
    else:
        c = by_word.astype(ml_dtypes.float4_e2m1fn).view(np.uint8) & 0xF
        words = (c[..., 0::2] | (c[..., 1::2] << 4)).reshape(k // 512, 128, 2 * n)
    return np.ascontiguousarray(words), np.ascontiguousarray(byte.astype(np.uint8).reshape(k // 512, 16, n))


def unpack_weight(words, scales, fmt):
    g, _, n = scales.shape
    words = np.ascontiguousarray(words).reshape(g, 128, n, -1)
    if fmt == "e4m3":
        vals = words.view(ml_dtypes.float8_e4m3fn).astype(np.float64)
    else:
        nib = np.empty((g, 128, n, 4), np.uint8)
        nib[..., 0::2] = words & 0xF
        nib[..., 1::2] = words >> 4
        vals = E2M1[nib]
    vals = vals * np.repeat(np.exp2(scales.astype(np.float64) - 127.0), 8, axis=1)[..., None]
    return vals.transpose(0, 1, 3, 2).reshape(g * 512, n)


def gelu(v):
    return 0.5 * v * (1.0 + np.tanh(np.sqrt(2.0 / np.pi) * (v + 0.044715 * v**3)))


K, T, S, K2, H, N = 1024, 4096, 1024, 512, 1024, 256


def setup_inputs():
    n = np.random.standard_normal
    s = mx_kscale(K)[:, None]
    s2 = mx_kscale(K2)[:, None]
    u = mx_kscale(H)[:, None]
    d = {}
    d["tab_words"], d["tab_scales"] = pack_weight(n((K, T)) * s, "e4m3")
    d["offs"] = striped(np.random.permutation(T)[:S])
    d["xs_words"], d["xs_scales"] = pack_weight(n((K2, S)) * s2, "e4m3")
    d["w1"] = (n((K, H)) / K ** 0.5 / s * u.T).astype(np.float32)
    d["w2_words"], d["w2_scales"] = pack_weight(n((K2, H)) / K2 ** 0.5 / s2 * u.T, "e2m1")
    d["por"] = np.exp(0.5 * n((H, S))).astype(np.float32)
    d["lamp"] = np.exp(0.4 * n(H)).astype(np.float32)
    d["w3"] = (n((H, N)) / H ** 0.5 / u).astype(np.float32)
    return d


def reference(tab_words, tab_scales, offs, xs_words, xs_scales, w1, w2_words, w2_scales, por, lamp, w3):
    v = unpack_weight(tab_words, tab_scales, "e4m3")[:, unstriped(offs)]
    xs = unpack_weight(xs_words, xs_scales, "e4m3")
    w2 = unpack_weight(w2_words, w2_scales, "e2m1")
    dye = mxq(f64(w1), 0, "e4m3").T @ v
    strand = w2.T @ xs
    h = np.abs(dye * f64(por) - f64(lamp)[:, None] * strand)
    out = mxq(f64(w3), 0, "e4m3").T @ mxq(h, 0, "e4m3")
    return out

@@ -1,0 +1,298 @@
+from contextlib import ExitStack
+
+import concourse.mybir as mybir
+from concourse.masks import make_identity
+
+K, T, S, K2, H, N = 1024, 4096, 1024, 512, 1024, 256
+FLOPS = 2 * S * (K * H + K2 * H + H * N)
+
+F32 = mybir.dt.float32
+BF16 = mybir.dt.bfloat16
+I32 = mybir.dt.int32
+U32 = mybir.dt.uint32
+U16 = mybir.dt.uint16
+U8 = mybir.dt.uint8
+FP8X4 = mybir.dt.float8_e4m3fn_x4
+FP4X4 = mybir.dt.float4_e2m1fn_x4
+MULT = mybir.AluOpType.mult
+SUB = mybir.AluOpType.subtract
+ABS = mybir.ActivationFunctionType.Abs
+
+P = 128
+PACK = 4
+PASS = P * PACK
+HALF = 512
+PIECE = 256
+
+
+def tile_list_shade_mismatch_step_kernel(
+    tc, tab_words, tab_scales, offs, xs_words, xs_scales, w1, w2_words, w2_scales, por, lamp, w3, out
+):
+    nc = tc.nc
+    with ExitStack() as ctx:
+        keep = ctx.enter_context(tc.tile_pool(name="keep", bufs=1))
+        ring = ctx.enter_context(tc.tile_pool(name="ring", bufs=3))
+        dye_ps = ctx.enter_context(tc.psum_pool(name="dye_ps", bufs=3))
+        strand_ps = ctx.enter_context(tc.psum_pool(name="strand_ps", bufs=3))
+        out_ps = ctx.enter_context(tc.psum_pool(name="out_ps", bufs=2))
+
+        def held(shape, dtype, name, tag=None):
+            return keep.tile(shape, dtype, name=name, tag=tag or name, align_bytes=64)
+
+        offsets = keep.tile([P, S // 16], U16, name="offsets")
+        nc.sync.dma_start(offsets[:], offs)
+
+        tab_plane = held([P, T], U8, "tab_plane")
+        w2_sc = held([P, H], U8, "w2_sc")
+        xs_plane = held([P, S], U8, "xs_plane")
+        nc.gpsimd.memset(tab_plane[:].bitcast(I32), 0)
+        for plane in (w2_sc, xs_plane):
+            nc.vector.memset(plane[:].bitcast(I32), 0)
+        for quad in range(4):
+            nc.gpsimd.dma_start(
+                tab_plane[32 * quad : 32 * quad + 8, :].bitcast(I32),
+                tab_scales[:, 4 * quad : 4 * quad + 4, :].bitcast(I32),
+            )
+
+        tab_sb = [held([P, T], I32, "tab%d" % a) for a in range(2)]
+
+        def load_tab(a, lo, hi):
+            src = tab_words[a].rearrange("p t i -> p (t i)")[:, 4 * lo : 4 * hi]
+            nc.sync.dma_start(tab_sb[a][:, lo:hi], src.bitcast(I32))
+
+        def load_w1(b, a):
+            raw = held([P, PACK, PASS], F32, "w1raw%d%d" % (b, a))
+            rows = w1[PASS * a : PASS * (a + 1), PASS * b : PASS * (b + 1)]
+            nc.sync.dma_start(raw[:], rows.rearrange("(p i) r -> p i r", i=PACK))
+            return raw
+
+        def load_xs(half):
+            words = held([P, HALF], I32, "xs%d" % half)
+            src = xs_words[0].rearrange("p c i -> p (c i)")[:, 4 * HALF * half : 4 * HALF * (half + 1)]
+            nc.sync.dma_start(words[:], src.bitcast(I32))
+            return words
+
+        def load_por(b, half, t):
+            tile = held([P, HALF], F32, "por%d%d%d" % (b, half, t))
+            rows = por[PASS * b : PASS * (b + 1), HALF * half : HALF * (half + 1)]
+            nc.sync.dma_start(tile[:], rows.rearrange("(q t i) j -> t q i j", t=PACK, i=8)[t])
+            return tile
+
+        def load_w3(b):
+            raw = held([P, PACK, N], F32, "w3raw%d" % b)
+            rows = w3[PASS * b : PASS * (b + 1), :].rearrange("(q t i) n -> t q i n", t=PACK, i=8)
+            for t in range(PACK):
+                nc.sync.dma_start(raw[:, t, :], rows[t])
+            return raw
+
+        w2_rows = held([P, H // 4], I32, "w2_rows")
+        xs_rows = held([P, S // 4], I32, "xs_rows")
+
+        def load_scale_rows(tile, rows, quad):
+            nc.sync.dma_start(
+                tile[32 * quad : 32 * quad + 4, :], rows[0, 4 * quad : 4 * quad + 4, :].bitcast(I32)
+            )
+
+        load_tab(0, 0, T // 4)
+        for quad in range(4):
+            load_scale_rows(w2_rows, w2_scales, quad)
+        lamp_raw = held([P, P], F32, "lamp_raw")
+        for b in range(2):
+            nc.sync.dma_start(
+                lamp_raw[PACK * b : PACK * (b + 1), :].rearrange("t (q i) -> t q i", i=8),
+                lamp[PASS * b : PASS * (b + 1)].rearrange("(q t i) -> t q i", t=PACK, i=8),
+            )
+        load_tab(0, T // 4, T // 2)
+        for quad in range(4):
+            load_scale_rows(xs_rows, xs_scales, quad)
+        w2_raw = held([P, H // 2], I32, "w2_raw")
+        nc.sync.dma_start(w2_raw[:], w2_words[0].bitcast(I32))
+        load_tab(0, T // 2, T)
+        load_tab(1, 0, T)
+        w1_raw = {(0, 0): load_w1(0, 0), (0, 1): load_w1(0, 1)}
+        xs_sb = [load_xs(0)]
+        por_sb = {}
+        for t in range(PACK):
+            por_sb[(0, 0, t)] = load_por(0, 0, t)
+        xs_sb.append(load_xs(1))
+        por_sb[(0, 1, 0)] = load_por(0, 1, 0)
+        w1_raw[(1, 0)] = load_w1(1, 0)
+        for t in range(1, PACK):
+            por_sb[(0, 1, t)] = load_por(0, 1, t)
+        w1_raw[(1, 1)] = load_w1(1, 1)
+        for t in range(PACK):
+            por_sb[(1, 0, t)] = load_por(1, 0, t)
+        w3_raw = [load_w3(0), load_w3(1)]
+        for t in range(PACK):
+            por_sb[(1, 1, t)] = load_por(1, 1, t)
+
+        w2_codes = held([P, 2 * H], U8, "w2_codes")
+        for quad in range(4):
+            live = slice(32 * quad, 32 * quad + 4)
+            nc.vector.tensor_copy(
+                w2_sc[live, :].bitcast(I32).rearrange("p (b t q e) -> p b t q e", b=2, t=PACK, e=2),
+                w2_rows[live, :].rearrange("p (b q t e) -> p b t q e", b=2, t=PACK, e=2),
+            )
+            nc.vector.tensor_copy(xs_plane[live, :].bitcast(I32), xs_rows[live, :])
+        nc.vector.tensor_copy(
+            w2_codes[:].bitcast(I32).rearrange("p (b t q e) -> p b t q e", b=2, t=PACK, e=4),
+            w2_raw[:].rearrange("p (b q t e) -> p b t q e", b=2, t=PACK, e=4),
+        )
+
+        lamp_rows = held([P, P], F32, "lamp_rows")
+        nc.vector.memset(lamp_rows[:], 0.0)
+        nc.vector.tensor_copy(lamp_rows[0 : 2 * PACK, :], lamp_raw[0 : 2 * PACK, :])
+        ident = held([P, P], F32, "ident")
+        make_identity(nc, ident[:])
+        turned = out_ps.tile([P, P], F32, name="acc")
+        nc.tensor.transpose(turned[:], lamp_rows[:], ident[:])
+        gains = held([P, 2 * PACK], F32, "gains")
+        nc.vector.tensor_copy(gains[:], turned[:, 0 : 2 * PACK])
+
+        v_plane = held([P, S], U8, "v_plane")
+        nc.vector.tensor_copy(v_plane[:], tab_plane[:].indirect(offsets[:]))
+        v_words = []
+        for a in range(2):
+            words = held([P, S], U32, "v%d" % a, tag="tab_plane" if a == 1 else None)
+            nc.vector.tensor_copy(words[:], tab_sb[a][:].bitcast(U32).indirect(offsets[:]))
+            v_words.append(words)
+
+        w1_q = {}
+
+        def round_w1(grouped, b, a, t, on_vector):
+            src = w1_raw[(b, a)][:].rearrange("p i (q t h e) -> p t q h i e", t=PACK, h=2, e=4)[:, t]
+            dst = grouped.rearrange("p (q h e i) -> p q h i e", h=2, e=4, i=PACK)
+            if on_vector:
+                nc.vector.tensor_copy(dst, src)
+            else:
+                nc.scalar.copy(dst, src)
+
+        def quantize(grouped, name):
+            width = grouped[:].shape[1] // PACK
+            codes = held([P, width], U32, name + "c")
+            scales = held([P, width], U8, name + "s")
+            nc.vector.quantize_mx(out=codes[:].bitcast(FP8X4), scales=scales[:], in_=grouped[:])
+            return codes, scales
+
+        def w1_whole(b, a):
+            grouped = held([P, PACK * PASS], BF16, "w1bf%d%d" % (b, a))
+            for t in range(PACK):
+                round_w1(grouped[:, PASS * t : PASS * (t + 1)], b, a, t, False)
+            codes, scales = quantize(grouped, "w1q%d%d" % (b, a))
+            for t in range(PACK):
+                w1_q[(b, a, t)] = (codes[:, P * t : P * (t + 1)], scales[:, P * t : P * (t + 1)])
+
+        w1_whole(0, 0)
+        slots = []
+        for t in range(PACK):
+            grouped = held([P, PASS], BF16, "w1bf01%d" % t)
+            round_w1(grouped[:], 0, 1, t, t == 0)
+            slots.append(grouped)
+        for t in range(PACK):
+            codes, scales = quantize(slots[t], "w1q01%d" % t)
+            w1_q[(0, 1, t)] = (codes[:], scales[:])
+
+        diff = {}
+        h_q = {}
+        w3_q = []
+
+        def products(b, t, c0, width):
+            half, lo = divmod(c0, HALF)
+            dye = dye_ps.tile([P, width], F32, name="dye")
+            for a in range(2):
+                codes, scales = w1_q[(b, a, t)]
+                nc.tensor.matmul_mx(
+                    out=dye[:],
+                    lhsT=codes.bitcast(FP8X4),
+                    lhsT_scale=scales,
+                    rhs=v_words[a][:, c0 : c0 + width].bitcast(FP8X4),
+                    rhs_scale=v_plane[4 * a : P, c0 : c0 + width],
+                    start=(a == 0),
+                    stop=(a == 1),
+                )
+            strand = strand_ps.tile([P, width], F32, name="strand")
+            col = PASS * b + P * t
+            nc.tensor.matmul_mx(
+                out=strand[:],
+                lhsT=w2_codes[:, 2 * col : 2 * (col + P)].bitcast(FP4X4),
+                lhsT_scale=w2_sc[:, col : col + P],
+                rhs=xs_sb[half][:, lo : lo + width].bitcast(FP8X4),
+                rhs_scale=xs_plane[:, c0 : c0 + width],
+                start=True,
+                stop=True,
+            )
+            weighted = ring.tile([P, width], F32, name="weighted")
+            nc.vector.tensor_tensor(weighted[:], dye[:], por_sb[(b, half, t)][:, lo : lo + width], MULT)
+            return strand, weighted
+
+        def difference(b, t, c0, width, strand, weighted):
+            if t == 0:
+                diff[(b, c0)] = held([P, PACK, width], F32, "diff%d_%d" % (b, c0))
+            nc.vector.scalar_tensor_tensor(
+                diff[(b, c0)][:, t, :], strand[:], gains[:, PACK * b + t : PACK * b + t + 1], weighted[:], MULT, SUB
+            )
+
+        def magnitude(b, c0, width):
+            grouped = held([P, width * PACK], BF16, "hbf%d_%d" % (b, c0))
+            for lo in range(0, width, PIECE):
+                nc.scalar.activation(
+                    grouped[:, PACK * lo : PACK * (lo + PIECE)].rearrange("p (c e t) -> p c t e", e=4, t=PACK),
+                    diff[(b, c0)][:, :, lo : lo + PIECE].rearrange("p t (c e) -> p c t e", e=4),
+                    ABS,
+                )
+            return grouped
+
+        def quantize_h(b, c0, width, grouped):
+            codes, scales = quantize(grouped, "hq%d_%d" % (b, c0))
+            for lo in range(0, width, PIECE):
+                h_q[(b, c0 + lo)] = (codes[:, lo : lo + PIECE], scales[:, lo : lo + PIECE])
+            if b == 1:
+                for lo in range(0, width, PIECE):
+                    scores(c0 + lo)
+
+        def scores(c0):
+            acc = out_ps.tile([P, 2, PIECE], F32, name="acc")
+            for nt in range(2):
+                for b in range(2):
+                    nc.tensor.matmul_mx(
+                        out=acc[:, nt, :],
+                        lhsT=w3_q[0][:, N * b + P * nt : N * b + P * (nt + 1)].bitcast(FP8X4),
+                        lhsT_scale=w3_q[1][:, N * b + P * nt : N * b + P * (nt + 1)],
+                        rhs=h_q[(b, c0)][0].bitcast(FP8X4),
+                        rhs_scale=h_q[(b, c0)][1],
+                        start=(b == 0),
+                        stop=(b == 1),
+                    )
+            staged = held([P, 2, PIECE], F32, "staged%d" % c0)
+            nc.scalar.copy(staged[:], acc[:])
+            nc.sync.dma_start(out.rearrange("(c p) j -> p c j", p=P)[:, :, c0 : c0 + PIECE], staged[:])
+
+        def w3_whole():
+            grouped = held([P, 2 * N * PACK], BF16, "w3bf")
+            for b in range(2):
+                nc.scalar.copy(
+                    grouped[:, N * PACK * b : N * PACK * (b + 1)].rearrange("p (c e t) -> p c t e", e=4, t=PACK),
+                    w3_raw[b][:].rearrange("p t (c e) -> p c t e", e=4),
+                )
+            w3_q.extend(quantize(grouped, "w3q"))
+
+        groups = [(0, 0, HALF), (0, HALF, HALF), (1, 0, HALF), (1, HALF, PIECE), (1, HALF + PIECE, PIECE)]
+        steps = [(b, t, c0, width) for (b, c0, width) in groups for t in range(PACK)]
+        before = None
+        waiting = None
+        for n, step in enumerate(steps + [None]):
+            made = products(*step) if step is not None else None
+            if before is not None:
+                difference(*before)
+                b, t, c0, width = before[:4]
+                if waiting is not None and t == 1:
+                    quantize_h(*waiting)
+                    waiting = None
+                if t == PACK - 1:
+                    waiting = (b, c0, width, magnitude(b, c0, width))
+            if n in (5, 7):
+                w1_whole(1, (n - 5) // 2)
+            if n == 11:
+                w3_whole()
+            before = step + made if step is not None else None
+        quantize_h(*waiting)

@@ -43,16 +43,12 @@ def tile_list_shade_mismatch_step_kernel(
         nc.sync.dma_start(offsets[:], offs)
 
         tab_plane = held([P, T], U8, "tab_plane")
-        w2_sc = held([P, H], U8, "w2_sc")
+        w2_plane = held([P, H], U8, "w2_plane")
         xs_plane = held([P, S], U8, "xs_plane")
-        nc.gpsimd.memset(tab_plane[:].bitcast(I32), 0)
-        for plane in (w2_sc, xs_plane):
+        lamp_rows = held([P, P], F32, "lamp_rows")
+        for plane in (tab_plane, w2_plane, xs_plane):
             nc.vector.memset(plane[:].bitcast(I32), 0)
-        for quad in range(4):
-            nc.gpsimd.dma_start(
-                tab_plane[32 * quad : 32 * quad + 8, :].bitcast(I32),
-                tab_scales[:, 4 * quad : 4 * quad + 4, :].bitcast(I32),
-            )
+        nc.vector.memset(lamp_rows[:], 0.0)
 
         tab_sb = [held([P, T], I32, "tab%d" % a) for a in range(2)]
 
@@ -85,77 +81,75 @@ def tile_list_shade_mismatch_step_kernel(
                 nc.sync.dma_start(raw[:, t, :], rows[t])
             return raw
 
-        w2_rows = held([P, H // 4], I32, "w2_rows")
-        xs_rows = held([P, S // 4], I32, "xs_rows")
-
-        def load_scale_rows(tile, rows, quad):
+        def load_scale_rows(plane, rows, a, quad):
+            first = 32 * quad + 4 * a
             nc.sync.dma_start(
-                tile[32 * quad : 32 * quad + 4, :], rows[0, 4 * quad : 4 * quad + 4, :].bitcast(I32)
+                plane[first : first + 4, :].bitcast(I32), rows[a, 4 * quad : 4 * quad + 4, :].bitcast(I32)
             )
 
-        load_tab(0, 0, T // 4)
+        load_tab(0, 0, 3 * T // 8)
+        for quad in range(3):
+            for a in range(2):
+                load_scale_rows(tab_plane, tab_scales, a, quad)
+        load_tab(0, 3 * T // 8, 5 * T // 8)
+        for a in range(2):
+            load_scale_rows(tab_plane, tab_scales, a, 3)
+        load_tab(0, 5 * T // 8, T)
         for quad in range(4):
-            load_scale_rows(w2_rows, w2_scales, quad)
-        lamp_raw = held([P, P], F32, "lamp_raw")
+            load_scale_rows(w2_plane, w2_scales, 0, quad)
+        load_tab(1, 0, T)
         for b in range(2):
             nc.sync.dma_start(
-                lamp_raw[PACK * b : PACK * (b + 1), :].rearrange("t (q i) -> t q i", i=8),
+                lamp_rows[PACK * b : PACK * (b + 1), :].rearrange("t (q i) -> t q i", i=8),
                 lamp[PASS * b : PASS * (b + 1)].rearrange("(q t i) -> t q i", t=PACK, i=8),
             )
-        load_tab(0, T // 4, T // 2)
-        for quad in range(4):
-            load_scale_rows(xs_rows, xs_scales, quad)
         w2_raw = held([P, H // 2], I32, "w2_raw")
         nc.sync.dma_start(w2_raw[:], w2_words[0].bitcast(I32))
-        load_tab(0, T // 2, T)
-        load_tab(1, 0, T)
-        w1_raw = {(0, 0): load_w1(0, 0), (0, 1): load_w1(0, 1)}
+        w1_raw = {(0, 0): load_w1(0, 0)}
+        for quad in range(4):
+            load_scale_rows(xs_plane, xs_scales, 0, quad)
         xs_sb = [load_xs(0)]
+        w1_raw[(0, 1)] = load_w1(0, 1)
         por_sb = {}
         for t in range(PACK):
             por_sb[(0, 0, t)] = load_por(0, 0, t)
-        xs_sb.append(load_xs(1))
-        por_sb[(0, 1, 0)] = load_por(0, 1, 0)
         w1_raw[(1, 0)] = load_w1(1, 0)
-        for t in range(1, PACK):
+        xs_sb.append(load_xs(1))
+        for t in range(2):
             por_sb[(0, 1, t)] = load_por(0, 1, t)
         w1_raw[(1, 1)] = load_w1(1, 1)
+        for t in range(2, PACK):
+            por_sb[(0, 1, t)] = load_por(0, 1, t)
         for t in range(PACK):
             por_sb[(1, 0, t)] = load_por(1, 0, t)
         w3_raw = [load_w3(0), load_w3(1)]
         for t in range(PACK):
             por_sb[(1, 1, t)] = load_por(1, 1, t)
 
+        v_plane = held([P, S], U8, "v_plane")
+        nc.vector.tensor_copy(v_plane[:], tab_plane[:].indirect(offsets[:]))
+        v_words = []
+        for a in range(2):
+            words = held([P, S], U32, "v%d" % a)
+            nc.vector.tensor_copy(words[:], tab_sb[a][:].bitcast(U32).indirect(offsets[:]))
+            v_words.append(words)
+
         w2_codes = held([P, 2 * H], U8, "w2_codes")
-        for quad in range(4):
-            live = slice(32 * quad, 32 * quad + 4)
-            nc.vector.tensor_copy(
-                w2_sc[live, :].bitcast(I32).rearrange("p (b t q e) -> p b t q e", b=2, t=PACK, e=2),
-                w2_rows[live, :].rearrange("p (b q t e) -> p b t q e", b=2, t=PACK, e=2),
-            )
-            nc.vector.tensor_copy(xs_plane[live, :].bitcast(I32), xs_rows[live, :])
+        w2_sc = held([P, H], U8, "w2_sc")
+        nc.vector.tensor_copy(
+            w2_sc[:].bitcast(I32).rearrange("p (b t q e) -> p b t q e", b=2, t=PACK, e=2),
+            w2_plane[:].bitcast(I32).rearrange("p (b q t e) -> p b t q e", b=2, t=PACK, e=2),
+        )
         nc.vector.tensor_copy(
             w2_codes[:].bitcast(I32).rearrange("p (b t q e) -> p b t q e", b=2, t=PACK, e=4),
             w2_raw[:].rearrange("p (b q t e) -> p b t q e", b=2, t=PACK, e=4),
         )
-
-        lamp_rows = held([P, P], F32, "lamp_rows")
-        nc.vector.memset(lamp_rows[:], 0.0)
-        nc.vector.tensor_copy(lamp_rows[0 : 2 * PACK, :], lamp_raw[0 : 2 * PACK, :])
         ident = held([P, P], F32, "ident")
         make_identity(nc, ident[:])
         turned = out_ps.tile([P, P], F32, name="acc")
         nc.tensor.transpose(turned[:], lamp_rows[:], ident[:])
         gains = held([P, 2 * PACK], F32, "gains")
         nc.vector.tensor_copy(gains[:], turned[:, 0 : 2 * PACK])
-
-        v_plane = held([P, S], U8, "v_plane")
-        nc.vector.tensor_copy(v_plane[:], tab_plane[:].indirect(offsets[:]))
-        v_words = []
-        for a in range(2):
-            words = held([P, S], U32, "v%d" % a, tag="tab_plane" if a == 1 else None)
-            nc.vector.tensor_copy(words[:], tab_sb[a][:].bitcast(U32).indirect(offsets[:]))
-            v_words.append(words)
 
         w1_q = {}
 
@@ -167,49 +161,54 @@ def tile_list_shade_mismatch_step_kernel(
             else:
                 nc.scalar.copy(dst, src)
 
-        def quantize(grouped, name):
+        def quantize(grouped, name, tag=None):
             width = grouped[:].shape[1] // PACK
-            codes = held([P, width], U32, name + "c")
+            codes = held([P, width], U32, name + "c", tag)
             scales = held([P, width], U8, name + "s")
             nc.vector.quantize_mx(out=codes[:].bitcast(FP8X4), scales=scales[:], in_=grouped[:])
             return codes, scales
 
-        def w1_whole(b, a):
-            grouped = held([P, PACK * PASS], BF16, "w1bf%d%d" % (b, a))
+        def w1_whole(b, a, behind=None, codes_behind=None):
+            grouped = held([P, PACK * PASS], BF16, "w1bf%d%d" % (b, a), behind)
             for t in range(PACK):
                 round_w1(grouped[:, PASS * t : PASS * (t + 1)], b, a, t, False)
-            codes, scales = quantize(grouped, "w1q%d%d" % (b, a))
+            codes, scales = quantize(grouped, "w1q%d%d" % (b, a), codes_behind)
             for t in range(PACK):
                 w1_q[(b, a, t)] = (codes[:, P * t : P * (t + 1)], scales[:, P * t : P * (t + 1)])
 
-        w1_whole(0, 0)
-        slots = []
-        for t in range(PACK):
-            grouped = held([P, PASS], BF16, "w1bf01%d" % t)
-            round_w1(grouped[:], 0, 1, t, t == 0)
-            slots.append(grouped)
-        for t in range(PACK):
-            codes, scales = quantize(slots[t], "w1q01%d" % t)
-            w1_q[(0, 1, t)] = (codes[:], scales[:])
+        slots = {}
+
+        def quantize_slot(a, t):
+            codes, scales = quantize(slots[(a, t)], "w1q0%d%d" % (a, t))
+            w1_q[(0, a, t)] = (codes[:], scales[:])
+
+        for a in range(2):
+            for t in range(PACK):
+                behind = {(0, 0): "tab1", (1, 0): "w1bf001"}.get((a, t))
+                slots[(a, t)] = held([P, PASS], BF16, "w1bf0%d%d" % (a, t), behind)
+                round_w1(slots[(a, t)][:], 0, a, t, t < 2 - a)
+            if a == 0:
+                for t in range(PACK):
+                    quantize_slot(0, t)
 
         diff = {}
         h_q = {}
         w3_q = []
 
-        def products(b, t, c0, width):
+        def dye_pass(dye, a, b, t, c0, width):
+            codes, scales = w1_q[(b, a, t)]
+            nc.tensor.matmul_mx(
+                out=dye[:],
+                lhsT=codes.bitcast(FP8X4),
+                lhsT_scale=scales,
+                rhs=v_words[a][:, c0 : c0 + width].bitcast(FP8X4),
+                rhs_scale=v_plane[4 * a : P, c0 : c0 + width],
+                start=(a == 0),
+                stop=(a == 1),
+            )
+
+        def open_step(b, t, c0, width):
             half, lo = divmod(c0, HALF)
-            dye = dye_ps.tile([P, width], F32, name="dye")
-            for a in range(2):
-                codes, scales = w1_q[(b, a, t)]
-                nc.tensor.matmul_mx(
-                    out=dye[:],
-                    lhsT=codes.bitcast(FP8X4),
-                    lhsT_scale=scales,
-                    rhs=v_words[a][:, c0 : c0 + width].bitcast(FP8X4),
-                    rhs_scale=v_plane[4 * a : P, c0 : c0 + width],
-                    start=(a == 0),
-                    stop=(a == 1),
-                )
             strand = strand_ps.tile([P, width], F32, name="strand")
             col = PASS * b + P * t
             nc.tensor.matmul_mx(
@@ -221,6 +220,13 @@ def tile_list_shade_mismatch_step_kernel(
                 start=True,
                 stop=True,
             )
+            dye = dye_ps.tile([P, width], F32, name="dye")
+            dye_pass(dye, 0, b, t, c0, width)
+            return strand, dye
+
+        def weigh(strand, dye, b, t, c0, width):
+            half, lo = divmod(c0, HALF)
+            dye_pass(dye, 1, b, t, c0, width)
             weighted = ring.tile([P, width], F32, name="weighted")
             nc.vector.tensor_tensor(weighted[:], dye[:], por_sb[(b, half, t)][:, lo : lo + width], MULT)
             return strand, weighted
@@ -234,41 +240,45 @@ def tile_list_shade_mismatch_step_kernel(
 
         def magnitude(b, c0, width):
             grouped = held([P, width * PACK], BF16, "hbf%d_%d" % (b, c0))
-            for lo in range(0, width, PIECE):
+            piece = min(width, PIECE)
+            for lo in range(0, width, piece):
                 nc.scalar.activation(
-                    grouped[:, PACK * lo : PACK * (lo + PIECE)].rearrange("p (c e t) -> p c t e", e=4, t=PACK),
-                    diff[(b, c0)][:, :, lo : lo + PIECE].rearrange("p t (c e) -> p c t e", e=4),
+                    grouped[:, PACK * lo : PACK * (lo + piece)].rearrange("p (c e t) -> p c t e", e=4, t=PACK),
+                    diff[(b, c0)][:, :, lo : lo + piece].rearrange("p t (c e) -> p c t e", e=4),
                     ABS,
                 )
             return grouped
 
         def quantize_h(b, c0, width, grouped):
             codes, scales = quantize(grouped, "hq%d_%d" % (b, c0))
-            for lo in range(0, width, PIECE):
-                h_q[(b, c0 + lo)] = (codes[:, lo : lo + PIECE], scales[:, lo : lo + PIECE])
+            h_q[(b, c0)] = (codes, scales)
             if b == 1:
-                for lo in range(0, width, PIECE):
-                    scores(c0 + lo)
+                piece = min(width, PIECE)
+                for lo in range(0, width, piece):
+                    scores(c0, lo, piece)
 
-        def scores(c0):
-            acc = out_ps.tile([P, 2, PIECE], F32, name="acc")
+        def scores(c0, lo, piece):
+            first = HALF * (c0 // HALF)
+            spans = [(h_q[(0, first)], c0 - first + lo), (h_q[(1, c0)], lo)]
+            acc = out_ps.tile([P, 2, piece], F32, name="acc")
             for nt in range(2):
                 for b in range(2):
+                    (codes, scales), at = spans[b]
                     nc.tensor.matmul_mx(
                         out=acc[:, nt, :],
                         lhsT=w3_q[0][:, N * b + P * nt : N * b + P * (nt + 1)].bitcast(FP8X4),
                         lhsT_scale=w3_q[1][:, N * b + P * nt : N * b + P * (nt + 1)],
-                        rhs=h_q[(b, c0)][0].bitcast(FP8X4),
-                        rhs_scale=h_q[(b, c0)][1],
+                        rhs=codes[:, at : at + piece].bitcast(FP8X4),
+                        rhs_scale=scales[:, at : at + piece],
                         start=(b == 0),
                         stop=(b == 1),
                     )
-            staged = held([P, 2, PIECE], F32, "staged%d" % c0)
+            staged = held([P, 2, piece], F32, "staged%d" % (c0 + lo))
             nc.scalar.copy(staged[:], acc[:])
-            nc.sync.dma_start(out.rearrange("(c p) j -> p c j", p=P)[:, :, c0 : c0 + PIECE], staged[:])
+            nc.sync.dma_start(out.rearrange("(c p) j -> p c j", p=P)[:, :, c0 + lo : c0 + lo + piece], staged[:])
 
         def w3_whole():
-            grouped = held([P, 2 * N * PACK], BF16, "w3bf")
+            grouped = held([P, 2 * N * PACK], BF16, "w3bf", "por102")
             for b in range(2):
                 nc.scalar.copy(
                     grouped[:, N * PACK * b : N * PACK * (b + 1)].rearrange("p (c e t) -> p c t e", e=4, t=PACK),
@@ -276,12 +286,18 @@ def tile_list_shade_mismatch_step_kernel(
                 )
             w3_q.extend(quantize(grouped, "w3q"))
 
-        groups = [(0, 0, HALF), (0, HALF, HALF), (1, 0, HALF), (1, HALF, PIECE), (1, HALF + PIECE, PIECE)]
+        groups = [(0, 0, 512), (0, 512, 512), (1, 0, 512), (1, 512, 256), (1, 768, 128), (1, 896, 128)]
         steps = [(b, t, c0, width) for (b, c0, width) in groups for t in range(PACK)]
+        opened = [open_step(*step) for step in steps[:3]]
         before = None
         waiting = None
         for n, step in enumerate(steps + [None]):
-            made = products(*step) if step is not None else None
+            if step is not None:
+                if n >= 3:
+                    opened.append(open_step(*step))
+                if n < PACK:
+                    quantize_slot(1, n)
+                made = weigh(*opened[n], *step)
             if before is not None:
                 difference(*before)
                 b, t, c0, width = before[:4]
@@ -290,9 +306,11 @@ def tile_list_shade_mismatch_step_kernel(
                     waiting = None
                 if t == PACK - 1:
                     waiting = (b, c0, width, magnitude(b, c0, width))
-            if n in (5, 7):
-                w1_whole(1, (n - 5) // 2)
-            if n == 11:
+            if n == 2:
+                w1_whole(1, 0, "por002")
+            if n == 5:
+                w1_whole(1, 1, "por011")
+            if n == 10:
                 w3_whole()
             before = step + made if step is not None else None
         quantize_h(*waiting)

@@ -15,6 +15,7 @@ U8 = mybir.dt.uint8
 FP8X4 = mybir.dt.float8_e4m3fn_x4
 FP4X4 = mybir.dt.float4_e2m1fn_x4
 MULT = mybir.AluOpType.mult
+ADD = mybir.AluOpType.add
 SUB = mybir.AluOpType.subtract
 ABS = mybir.ActivationFunctionType.Abs
 
@@ -74,12 +75,9 @@ def tile_list_shade_mismatch_step_kernel(
             nc.sync.dma_start(tile[:], rows.rearrange("(q t i) j -> t q i j", t=PACK, i=8)[t])
             return tile
 
-        def load_w3(b):
-            raw = held([P, PACK, N], F32, "w3raw%d" % b)
+        def load_w3(b, t):
             rows = w3[PASS * b : PASS * (b + 1), :].rearrange("(q t i) n -> t q i n", t=PACK, i=8)
-            for t in range(PACK):
-                nc.sync.dma_start(raw[:, t, :], rows[t])
-            return raw
+            nc.sync.dma_start(w3_raw[b][:, t, :], rows[t])
 
         def load_scale_rows(plane, rows, a, quad):
             first = 32 * quad + 4 * a
@@ -120,9 +118,11 @@ def tile_list_shade_mismatch_step_kernel(
         w1_raw[(1, 1)] = load_w1(1, 1)
         for t in range(2, PACK):
             por_sb[(0, 1, t)] = load_por(0, 1, t)
+        w3_raw = [held([P, PACK, N], F32, "w3raw%d" % b) for b in range(2)]
         for t in range(PACK):
             por_sb[(1, 0, t)] = load_por(1, 0, t)
-        w3_raw = [load_w3(0), load_w3(1)]
+            for b in range(2):
+                load_w3(b, t)
         for t in range(PACK):
             por_sb[(1, 1, t)] = load_por(1, 1, t)
 
@@ -154,8 +154,8 @@ def tile_list_shade_mismatch_step_kernel(
         w1_q = {}
 
         def round_w1(grouped, b, a, t, on_vector):
-            src = w1_raw[(b, a)][:].rearrange("p i (q t h e) -> p t q h i e", t=PACK, h=2, e=4)[:, t]
-            dst = grouped.rearrange("p (q h e i) -> p q h i e", h=2, e=4, i=PACK)
+            src = w1_raw[(b, a)][:].rearrange("p i (q t e) -> p t q e i", t=PACK, e=8)[:, t]
+            dst = grouped.rearrange("p (q e i) -> p q e i", e=8, i=PACK)
             if on_vector:
                 nc.vector.tensor_copy(dst, src)
             else:
@@ -168,11 +168,15 @@ def tile_list_shade_mismatch_step_kernel(
             nc.vector.quantize_mx(out=codes[:].bitcast(FP8X4), scales=scales[:], in_=grouped[:])
             return codes, scales
 
-        def w1_whole(b, a, behind=None, codes_behind=None):
-            grouped = held([P, PACK * PASS], BF16, "w1bf%d%d" % (b, a), behind)
+        w1_bf = {}
+
+        def round_w1_pass(b, a, behind):
+            w1_bf[(b, a)] = held([P, PACK * PASS], BF16, "w1bf%d%d" % (b, a), behind)
             for t in range(PACK):
-                round_w1(grouped[:, PASS * t : PASS * (t + 1)], b, a, t, False)
-            codes, scales = quantize(grouped, "w1q%d%d" % (b, a), codes_behind)
+                round_w1(w1_bf[(b, a)][:, PASS * t : PASS * (t + 1)], b, a, t, False)
+
+        def quantize_w1_pass(b, a, behind):
+            codes, scales = quantize(w1_bf[(b, a)], "w1q%d%d" % (b, a), behind)
             for t in range(PACK):
                 w1_q[(b, a, t)] = (codes[:, P * t : P * (t + 1)], scales[:, P * t : P * (t + 1)])
 
@@ -192,6 +196,7 @@ def tile_list_shade_mismatch_step_kernel(
                     quantize_slot(0, t)
 
         diff = {}
+        h_bf = {}
         h_q = {}
         w3_q = []
 
@@ -238,32 +243,27 @@ def tile_list_shade_mismatch_step_kernel(
                 diff[(b, c0)][:, t, :], strand[:], gains[:, PACK * b + t : PACK * b + t + 1], weighted[:], MULT, SUB
             )
 
-        def magnitude(b, c0, width):
-            grouped = held([P, width * PACK], BF16, "hbf%d_%d" % (b, c0))
+        def magnitude(b, c0, lo, width, behind=None):
+            grouped = held([P, width * PACK], BF16, "hbf%d_%d" % (b, c0 + lo), behind)
             piece = min(width, PIECE)
-            for lo in range(0, width, piece):
+            for at in range(0, width, piece):
                 nc.scalar.activation(
-                    grouped[:, PACK * lo : PACK * (lo + piece)].rearrange("p (c e t) -> p c t e", e=4, t=PACK),
-                    diff[(b, c0)][:, :, lo : lo + piece].rearrange("p t (c e) -> p c t e", e=4),
+                    grouped[:, PACK * at : PACK * (at + piece)].rearrange("p (j t) -> p j t", t=PACK),
+                    diff[(b, c0)][:, :, lo + at : lo + at + piece].rearrange("p t j -> p j t"),
                     ABS,
                 )
-            return grouped
+            h_bf[(b, c0 + lo)] = grouped
 
-        def quantize_h(b, c0, width, grouped):
-            codes, scales = quantize(grouped, "hq%d_%d" % (b, c0))
-            h_q[(b, c0)] = (codes, scales)
-            if b == 1:
-                piece = min(width, PIECE)
-                for lo in range(0, width, piece):
-                    scores(c0, lo, piece)
+        def quantize_h(b, c0, behind=None):
+            codes, scales = quantize(h_bf[(b, c0)], "hq%d_%d" % (b, c0), behind)
+            for lo in range(0, codes[:].shape[1], P):
+                h_q[(b, c0 + lo)] = (codes, scales, lo)
 
-        def scores(c0, lo, piece):
-            first = HALF * (c0 // HALF)
-            spans = [(h_q[(0, first)], c0 - first + lo), (h_q[(1, c0)], lo)]
+        def scores(c0, piece):
             acc = out_ps.tile([P, 2, piece], F32, name="acc")
             for nt in range(2):
                 for b in range(2):
-                    (codes, scales), at = spans[b]
+                    codes, scales, at = h_q[(b, c0)]
                     nc.tensor.matmul_mx(
                         out=acc[:, nt, :],
                         lhsT=w3_q[0][:, N * b + P * nt : N * b + P * (nt + 1)].bitcast(FP8X4),
@@ -273,24 +273,30 @@ def tile_list_shade_mismatch_step_kernel(
                         start=(b == 0),
                         stop=(b == 1),
                     )
-            staged = held([P, 2, piece], F32, "staged%d" % (c0 + lo))
+            staged = held([P, 2, piece], F32, "staged%d" % c0)
             nc.scalar.copy(staged[:], acc[:])
-            nc.sync.dma_start(out.rearrange("(c p) j -> p c j", p=P)[:, :, c0 + lo : c0 + lo + piece], staged[:])
+            nc.sync.dma_start(out.rearrange("(c p) j -> p c j", p=P)[:, :, c0 : c0 + piece], staged[:])
 
-        def w3_whole():
-            grouped = held([P, 2 * N * PACK], BF16, "w3bf", "por102")
+        w3_bf = []
+
+        def round_w3():
+            grouped = held([P, 2 * N * PACK], BF16, "w3bf")
             for b in range(2):
-                nc.scalar.copy(
-                    grouped[:, N * PACK * b : N * PACK * (b + 1)].rearrange("p (c e t) -> p c t e", e=4, t=PACK),
-                    w3_raw[b][:].rearrange("p t (c e) -> p c t e", e=4),
+                nc.gpsimd.tensor_scalar(
+                    grouped[:, N * PACK * b : N * PACK * (b + 1)].rearrange("p (n t) -> p n t", t=PACK),
+                    w3_raw[b][:].rearrange("p t n -> p n t"),
+                    1.0,
+                    0.0,
+                    MULT,
+                    ADD,
                 )
-            w3_q.extend(quantize(grouped, "w3q"))
+            w3_bf.append(grouped)
 
         groups = [(0, 0, 512), (0, 512, 512), (1, 0, 512), (1, 512, 256), (1, 768, 128), (1, 896, 128)]
         steps = [(b, t, c0, width) for (b, c0, width) in groups for t in range(PACK)]
+        round_w3()
         opened = [open_step(*step) for step in steps[:3]]
         before = None
-        waiting = None
         for n, step in enumerate(steps + [None]):
             if step is not None:
                 if n >= 3:
@@ -300,17 +306,35 @@ def tile_list_shade_mismatch_step_kernel(
                 made = weigh(*opened[n], *step)
             if before is not None:
                 difference(*before)
-                b, t, c0, width = before[:4]
-                if waiting is not None and t == 1:
-                    quantize_h(*waiting)
-                    waiting = None
-                if t == PACK - 1:
-                    waiting = (b, c0, width, magnitude(b, c0, width))
             if n == 2:
-                w1_whole(1, 0, "por002")
+                round_w1_pass(1, 0, "por002")
+            if n == 4:
+                magnitude(0, 0, 0, PIECE)
             if n == 5:
-                w1_whole(1, 1, "por011")
-            if n == 10:
-                w3_whole()
+                round_w1_pass(1, 1, "por011")
+                magnitude(0, 0, PIECE, PIECE, "w1raw11")
+            if n == 6:
+                quantize_w1_pass(1, 0, "por012")
+            if n == 7:
+                quantize_w1_pass(1, 1, None)
+            if n == 8:
+                magnitude(0, HALF, 0, HALF)
+            if n == 9:
+                quantize_h(0, 0, "por100")
+                quantize_h(0, PIECE, "por101")
+            if n == 11:
+                quantize_h(0, HALF, "por103")
+            if n == 12:
+                magnitude(1, 0, 0, HALF)
+                w3_q.extend(quantize(w3_bf[0], "w3q", "por102"))
+            if n == 15:
+                quantize_h(1, 0)
+                scores(0, PIECE)
+                scores(PIECE, PIECE)
+            if n in (16, 20, 24):
+                magnitude(1, before[2], 0, before[3])
+            if n in (18, 22, 24):
+                b, c0, width = groups[{18: 3, 22: 4, 24: 5}[n]]
+                quantize_h(b, c0)
+                scores(c0, width)
             before = step + made if step is not None else None
-        quantize_h(*waiting)

@@ -1,7 +1,6 @@
 from contextlib import ExitStack
 
 import concourse.mybir as mybir
-from concourse.masks import make_identity
 
 K, T, S, K2, H, N = 1024, 4096, 1024, 512, 1024, 256
 FLOPS = 2 * S * (K * H + K2 * H + H * N)
@@ -15,7 +14,6 @@ U8 = mybir.dt.uint8
 FP8X4 = mybir.dt.float8_e4m3fn_x4
 FP4X4 = mybir.dt.float4_e2m1fn_x4
 MULT = mybir.AluOpType.mult
-ADD = mybir.AluOpType.add
 SUB = mybir.AluOpType.subtract
 ABS = mybir.ActivationFunctionType.Abs
 
@@ -46,10 +44,8 @@ def tile_list_shade_mismatch_step_kernel(
         tab_plane = held([P, T], U8, "tab_plane")
         w2_plane = held([P, H], U8, "w2_plane")
         xs_plane = held([P, S], U8, "xs_plane")
-        lamp_rows = held([P, P], F32, "lamp_rows")
-        for plane in (tab_plane, w2_plane, xs_plane):
+        for plane in (w2_plane, tab_plane, xs_plane):
             nc.vector.memset(plane[:].bitcast(I32), 0)
-        nc.vector.memset(lamp_rows[:], 0.0)
 
         tab_sb = [held([P, T], I32, "tab%d" % a) for a in range(2)]
 
@@ -72,12 +68,13 @@ def tile_list_shade_mismatch_step_kernel(
         def load_por(b, half, t):
             tile = held([P, HALF], F32, "por%d%d%d" % (b, half, t))
             rows = por[PASS * b : PASS * (b + 1), HALF * half : HALF * (half + 1)]
-            nc.sync.dma_start(tile[:], rows.rearrange("(q t i) j -> t q i j", t=PACK, i=8)[t])
+            nc.sync.dma_start(tile[:], rows.rearrange("(p t) j -> t p j", t=PACK)[t])
             return tile
 
-        def load_w3(b, t):
-            rows = w3[PASS * b : PASS * (b + 1), :].rearrange("(q t i) n -> t q i n", t=PACK, i=8)
-            nc.sync.dma_start(w3_raw[b][:, t, :], rows[t])
+        def load_w3(b):
+            raw = held([P, PACK, N], F32, "w3raw%d" % b)
+            nc.sync.dma_start(raw[:], w3[PASS * b : PASS * (b + 1), :].rearrange("(p t) n -> p t n", t=PACK))
+            return raw
 
         def load_scale_rows(plane, rows, a, quad):
             first = 32 * quad + 4 * a
@@ -85,28 +82,25 @@ def tile_list_shade_mismatch_step_kernel(
                 plane[first : first + 4, :].bitcast(I32), rows[a, 4 * quad : 4 * quad + 4, :].bitcast(I32)
             )
 
-        load_tab(0, 0, 3 * T // 8)
-        for quad in range(3):
-            for a in range(2):
-                load_scale_rows(tab_plane, tab_scales, a, quad)
-        load_tab(0, 3 * T // 8, 5 * T // 8)
-        for a in range(2):
-            load_scale_rows(tab_plane, tab_scales, a, 3)
-        load_tab(0, 5 * T // 8, T)
+        w2_raw = held([P, 2 * H], U8, "w2_raw")
+        nc.sync.dma_start(w2_raw[:].bitcast(I32), w2_words[0].bitcast(I32))
         for quad in range(4):
             load_scale_rows(w2_plane, w2_scales, 0, quad)
+        tab_rows = [(a, quad) for quad in range(4) for a in range(2)]
+        load_tab(0, 0, 3 * T // 8)
+        for a, quad in tab_rows[:3]:
+            load_scale_rows(tab_plane, tab_scales, a, quad)
+        load_tab(0, 3 * T // 8, 6 * T // 8)
+        for a, quad in tab_rows[3:]:
+            load_scale_rows(tab_plane, tab_scales, a, quad)
+        load_tab(0, 6 * T // 8, T)
         load_tab(1, 0, T)
-        for b in range(2):
-            nc.sync.dma_start(
-                lamp_rows[PACK * b : PACK * (b + 1), :].rearrange("t (q i) -> t q i", i=8),
-                lamp[PASS * b : PASS * (b + 1)].rearrange("(q t i) -> t q i", t=PACK, i=8),
-            )
-        w2_raw = held([P, H // 2], I32, "w2_raw")
-        nc.sync.dma_start(w2_raw[:], w2_words[0].bitcast(I32))
-        w1_raw = {(0, 0): load_w1(0, 0)}
+        gains = held([P, 2, PACK], F32, "gains")
+        nc.sync.dma_start(gains[:], lamp.rearrange("(b p t) -> p b t", b=2, t=PACK))
         for quad in range(4):
             load_scale_rows(xs_plane, xs_scales, 0, quad)
         xs_sb = [load_xs(0)]
+        w1_raw = {(0, 0): load_w1(0, 0)}
         w1_raw[(0, 1)] = load_w1(0, 1)
         por_sb = {}
         for t in range(PACK):
@@ -118,13 +112,22 @@ def tile_list_shade_mismatch_step_kernel(
         w1_raw[(1, 1)] = load_w1(1, 1)
         for t in range(2, PACK):
             por_sb[(0, 1, t)] = load_por(0, 1, t)
-        w3_raw = [held([P, PACK, N], F32, "w3raw%d" % b) for b in range(2)]
         for t in range(PACK):
             por_sb[(1, 0, t)] = load_por(1, 0, t)
-            for b in range(2):
-                load_w3(b, t)
+        w3_raw = [load_w3(0), load_w3(1)]
         for t in range(PACK):
             por_sb[(1, 1, t)] = load_por(1, 1, t)
+
+        w2_codes = held([P, 2 * H], U8, "w2_codes")
+        w2_sc = held([P, H], U8, "w2_sc")
+        nc.vector.tensor_copy(
+            w2_codes[:].rearrange("p (b t m e) -> p b t m e", b=2, t=PACK, e=2),
+            w2_raw[:].rearrange("p (b m t e) -> p b t m e", b=2, t=PACK, e=2),
+        )
+        nc.vector.tensor_copy(
+            w2_sc[:].rearrange("p (b t m) -> p b t m", b=2, t=PACK),
+            w2_plane[:].rearrange("p (b m t) -> p b t m", b=2, t=PACK),
+        )
 
         v_plane = held([P, S], U8, "v_plane")
         nc.vector.tensor_copy(v_plane[:], tab_plane[:].indirect(offsets[:]))
@@ -134,66 +137,48 @@ def tile_list_shade_mismatch_step_kernel(
             nc.vector.tensor_copy(words[:], tab_sb[a][:].bitcast(U32).indirect(offsets[:]))
             v_words.append(words)
 
-        w2_codes = held([P, 2 * H], U8, "w2_codes")
-        w2_sc = held([P, H], U8, "w2_sc")
-        nc.vector.tensor_copy(
-            w2_sc[:].bitcast(I32).rearrange("p (b t q e) -> p b t q e", b=2, t=PACK, e=2),
-            w2_plane[:].bitcast(I32).rearrange("p (b q t e) -> p b t q e", b=2, t=PACK, e=2),
-        )
-        nc.vector.tensor_copy(
-            w2_codes[:].bitcast(I32).rearrange("p (b t q e) -> p b t q e", b=2, t=PACK, e=4),
-            w2_raw[:].rearrange("p (b q t e) -> p b t q e", b=2, t=PACK, e=4),
-        )
-        ident = held([P, P], F32, "ident")
-        make_identity(nc, ident[:])
-        turned = out_ps.tile([P, P], F32, name="acc")
-        nc.tensor.transpose(turned[:], lamp_rows[:], ident[:])
-        gains = held([P, 2 * PACK], F32, "gains")
-        nc.vector.tensor_copy(gains[:], turned[:, 0 : 2 * PACK])
-
         w1_q = {}
 
-        def round_w1(grouped, b, a, t, on_vector):
-            src = w1_raw[(b, a)][:].rearrange("p i (q t e) -> p t q e i", t=PACK, e=8)[:, t]
-            dst = grouped.rearrange("p (q e i) -> p q e i", e=8, i=PACK)
+        def round_w1(grouped, b, a, u, on_vector):
+            src = w1_raw[(b, a)][:].rearrange("p i (m u e) -> p u m i e", u=2, e=2)[:, u]
+            dst = grouped.rearrange("p (e m i) -> p m i e", e=2, i=PACK)
             if on_vector:
                 nc.vector.tensor_copy(dst, src)
             else:
                 nc.scalar.copy(dst, src)
 
         def quantize(grouped, name, tag=None):
-            width = grouped[:].shape[1] // PACK
+            width = grouped.shape[1] // PACK
             codes = held([P, width], U32, name + "c", tag)
             scales = held([P, width], U8, name + "s")
-            nc.vector.quantize_mx(out=codes[:].bitcast(FP8X4), scales=scales[:], in_=grouped[:])
+            nc.vector.quantize_mx(out=codes[:].bitcast(FP8X4), scales=scales[:], in_=grouped)
             return codes, scales
 
         w1_bf = {}
 
         def round_w1_pass(b, a, behind):
             w1_bf[(b, a)] = held([P, PACK * PASS], BF16, "w1bf%d%d" % (b, a), behind)
-            for t in range(PACK):
-                round_w1(w1_bf[(b, a)][:, PASS * t : PASS * (t + 1)], b, a, t, False)
+            for u in range(2):
+                round_w1(w1_bf[(b, a)][:, 2 * PASS * u : 2 * PASS * (u + 1)], b, a, u, False)
 
         def quantize_w1_pass(b, a, behind):
-            codes, scales = quantize(w1_bf[(b, a)], "w1q%d%d" % (b, a), behind)
+            codes, scales = quantize(w1_bf[(b, a)][:], "w1q%d%d" % (b, a), behind)
             for t in range(PACK):
                 w1_q[(b, a, t)] = (codes[:, P * t : P * (t + 1)], scales[:, P * t : P * (t + 1)])
 
-        slots = {}
-
-        def quantize_slot(a, t):
-            codes, scales = quantize(slots[(a, t)], "w1q0%d%d" % (a, t))
-            w1_q[(0, a, t)] = (codes[:], scales[:])
+        def quantize_pair(a, u):
+            codes, scales = quantize(w1_bf[(0, a, u)][:], "w1q0%d%d" % (a, u))
+            for e in range(2):
+                w1_q[(0, a, 2 * u + e)] = (codes[:, P * e : P * (e + 1)], scales[:, P * e : P * (e + 1)])
 
         for a in range(2):
-            for t in range(PACK):
-                behind = {(0, 0): "tab1", (1, 0): "w1bf001"}.get((a, t))
-                slots[(a, t)] = held([P, PASS], BF16, "w1bf0%d%d" % (a, t), behind)
-                round_w1(slots[(a, t)][:], 0, a, t, t < 2 - a)
+            for u in range(2):
+                behind = {(0, 0): "tab1", (1, 0): "w1raw00"}.get((a, u))
+                w1_bf[(0, a, u)] = held([P, 2 * PASS], BF16, "w1bf0%d%d" % (a, u), behind)
+                round_w1(w1_bf[(0, a, u)][:], 0, a, u, u == 0)
             if a == 0:
-                for t in range(PACK):
-                    quantize_slot(0, t)
+                for u in range(2):
+                    quantize_pair(0, u)
 
         diff = {}
         h_bf = {}
@@ -240,7 +225,7 @@ def tile_list_shade_mismatch_step_kernel(
             if t == 0:
                 diff[(b, c0)] = held([P, PACK, width], F32, "diff%d_%d" % (b, c0))
             nc.vector.scalar_tensor_tensor(
-                diff[(b, c0)][:, t, :], strand[:], gains[:, PACK * b + t : PACK * b + t + 1], weighted[:], MULT, SUB
+                diff[(b, c0)][:, t, :], strand[:], gains[:, b, t : t + 1], weighted[:], MULT, SUB
             )
 
         def magnitude(b, c0, lo, width, behind=None):
@@ -248,14 +233,14 @@ def tile_list_shade_mismatch_step_kernel(
             piece = min(width, PIECE)
             for at in range(0, width, piece):
                 nc.scalar.activation(
-                    grouped[:, PACK * at : PACK * (at + piece)].rearrange("p (j t) -> p j t", t=PACK),
-                    diff[(b, c0)][:, :, lo + at : lo + at + piece].rearrange("p t j -> p j t"),
+                    grouped[:, PACK * at : PACK * (at + piece)].rearrange("p (c e t) -> p c t e", e=4, t=PACK),
+                    diff[(b, c0)][:, :, lo + at : lo + at + piece].rearrange("p t (c e) -> p c t e", e=4),
                     ABS,
                 )
             h_bf[(b, c0 + lo)] = grouped
 
         def quantize_h(b, c0, behind=None):
-            codes, scales = quantize(h_bf[(b, c0)], "hq%d_%d" % (b, c0), behind)
+            codes, scales = quantize(h_bf[(b, c0)][:], "hq%d_%d" % (b, c0), behind)
             for lo in range(0, codes[:].shape[1], P):
                 h_q[(b, c0 + lo)] = (codes, scales, lo)
 
@@ -279,30 +264,25 @@ def tile_list_shade_mismatch_step_kernel(
 
         w3_bf = []
 
-        def round_w3():
-            grouped = held([P, 2 * N * PACK], BF16, "w3bf")
+        def round_w3(behind):
+            grouped = held([P, 2 * N * PACK], BF16, "w3bf", behind)
             for b in range(2):
-                nc.gpsimd.tensor_scalar(
-                    grouped[:, N * PACK * b : N * PACK * (b + 1)].rearrange("p (n t) -> p n t", t=PACK),
-                    w3_raw[b][:].rearrange("p t n -> p n t"),
-                    1.0,
-                    0.0,
-                    MULT,
-                    ADD,
+                nc.scalar.copy(
+                    grouped[:, N * PACK * b : N * PACK * (b + 1)].rearrange("p (c e t) -> p c t e", e=4, t=PACK),
+                    w3_raw[b][:].rearrange("p t (c e) -> p c t e", e=4),
                 )
             w3_bf.append(grouped)
 
         groups = [(0, 0, 512), (0, 512, 512), (1, 0, 512), (1, 512, 256), (1, 768, 128), (1, 896, 128)]
         steps = [(b, t, c0, width) for (b, c0, width) in groups for t in range(PACK)]
-        round_w3()
         opened = [open_step(*step) for step in steps[:3]]
         before = None
         for n, step in enumerate(steps + [None]):
             if step is not None:
                 if n >= 3:
                     opened.append(open_step(*step))
-                if n < PACK:
-                    quantize_slot(1, n)
+                if n in (0, 2):
+                    quantize_pair(1, n // 2)
                 made = weigh(*opened[n], *step)
             if before is not None:
                 difference(*before)
@@ -322,11 +302,14 @@ def tile_list_shade_mismatch_step_kernel(
             if n == 9:
                 quantize_h(0, 0, "por100")
                 quantize_h(0, PIECE, "por101")
+            if n == 10:
+                round_w3("por102")
             if n == 11:
                 quantize_h(0, HALF, "por103")
             if n == 12:
                 magnitude(1, 0, 0, HALF)
-                w3_q.extend(quantize(w3_bf[0], "w3q", "por102"))
+            if n == 13:
+                w3_q.extend(quantize(w3_bf[0][:], "w3q", "diff0_512"))
             if n == 15:
                 quantize_h(1, 0)
                 scores(0, PIECE)

from contextlib import ExitStack

import concourse.mybir as mybir

K, T, S, K2, H, N = 1024, 4096, 1024, 512, 1024, 256
FLOPS = 2 * S * (K * H + K2 * H + H * N)

F32 = mybir.dt.float32
BF16 = mybir.dt.bfloat16
I32 = mybir.dt.int32
U32 = mybir.dt.uint32
U16 = mybir.dt.uint16
U8 = mybir.dt.uint8
FP8X4 = mybir.dt.float8_e4m3fn_x4
FP4X4 = mybir.dt.float4_e2m1fn_x4
MULT = mybir.AluOpType.mult
SUB = mybir.AluOpType.subtract
ABS = mybir.ActivationFunctionType.Abs

P = 128
PACK = 4
PASS = P * PACK
HALF = 512
PIECE = 256


def tile_list_shade_mismatch_step_kernel(
    tc, tab_words, tab_scales, offs, xs_words, xs_scales, w1, w2_words, w2_scales, por, lamp, w3, out
):
    nc = tc.nc
    with ExitStack() as ctx:
        keep = ctx.enter_context(tc.tile_pool(name="keep", bufs=1))
        ring = ctx.enter_context(tc.tile_pool(name="ring", bufs=3))
        dye_ps = ctx.enter_context(tc.psum_pool(name="dye_ps", bufs=3))
        strand_ps = ctx.enter_context(tc.psum_pool(name="strand_ps", bufs=3))
        out_ps = ctx.enter_context(tc.psum_pool(name="out_ps", bufs=2))

        def held(shape, dtype, name, tag=None):
            return keep.tile(shape, dtype, name=name, tag=tag or name, align_bytes=64)

        offsets = keep.tile([P, S // 16], U16, name="offsets")
        nc.sync.dma_start(offsets[:], offs)

        tab_plane = held([P, T], U8, "tab_plane")
        w2_plane = held([P, H], U8, "w2_plane")
        xs_plane = held([P, S], U8, "xs_plane")
        for plane in (w2_plane, tab_plane, xs_plane):
            nc.vector.memset(plane[:].bitcast(I32), 0)

        tab_sb = [held([P, T], I32, "tab%d" % a) for a in range(2)]

        def load_tab(a, lo, hi):
            src = tab_words[a].rearrange("p t i -> p (t i)")[:, 4 * lo : 4 * hi]
            nc.sync.dma_start(tab_sb[a][:, lo:hi], src.bitcast(I32))

        def load_w1(b, a):
            raw = held([P, PACK, PASS], F32, "w1raw%d%d" % (b, a))
            rows = w1[PASS * a : PASS * (a + 1), PASS * b : PASS * (b + 1)]
            nc.sync.dma_start(raw[:], rows.rearrange("(p i) r -> p i r", i=PACK))
            return raw

        def load_xs(half):
            words = held([P, HALF], I32, "xs%d" % half)
            src = xs_words[0].rearrange("p c i -> p (c i)")[:, 4 * HALF * half : 4 * HALF * (half + 1)]
            nc.sync.dma_start(words[:], src.bitcast(I32))
            return words

        def load_por(b, half, t):
            tile = held([P, HALF], F32, "por%d%d%d" % (b, half, t))
            rows = por[PASS * b : PASS * (b + 1), HALF * half : HALF * (half + 1)]
            nc.sync.dma_start(tile[:], rows.rearrange("(p t) j -> t p j", t=PACK)[t])
            return tile

        def load_w3(b):
            raw = held([P, PACK, N], F32, "w3raw%d" % b)
            nc.sync.dma_start(raw[:], w3[PASS * b : PASS * (b + 1), :].rearrange("(p t) n -> p t n", t=PACK))
            return raw

        def load_scale_rows(plane, rows, a, quad):
            first = 32 * quad + 4 * a
            nc.sync.dma_start(
                plane[first : first + 4, :].bitcast(I32), rows[a, 4 * quad : 4 * quad + 4, :].bitcast(I32)
            )

        w2_raw = held([P, 2 * H], U8, "w2_raw")
        nc.sync.dma_start(w2_raw[:].bitcast(I32), w2_words[0].bitcast(I32))
        for quad in range(4):
            load_scale_rows(w2_plane, w2_scales, 0, quad)
        tab_rows = [(a, quad) for quad in range(4) for a in range(2)]
        load_tab(0, 0, 3 * T // 8)
        for a, quad in tab_rows[:3]:
            load_scale_rows(tab_plane, tab_scales, a, quad)
        load_tab(0, 3 * T // 8, 6 * T // 8)
        for a, quad in tab_rows[3:]:
            load_scale_rows(tab_plane, tab_scales, a, quad)
        load_tab(0, 6 * T // 8, T)
        load_tab(1, 0, T)
        gains = held([P, 2, PACK], F32, "gains")
        nc.sync.dma_start(gains[:], lamp.rearrange("(b p t) -> p b t", b=2, t=PACK))
        for quad in range(4):
            load_scale_rows(xs_plane, xs_scales, 0, quad)
        xs_sb = [load_xs(0)]
        w1_raw = {(0, 0): load_w1(0, 0)}
        w1_raw[(0, 1)] = load_w1(0, 1)
        por_sb = {}
        for t in range(PACK):
            por_sb[(0, 0, t)] = load_por(0, 0, t)
        w1_raw[(1, 0)] = load_w1(1, 0)
        xs_sb.append(load_xs(1))
        for t in range(2):
            por_sb[(0, 1, t)] = load_por(0, 1, t)
        w1_raw[(1, 1)] = load_w1(1, 1)
        for t in range(2, PACK):
            por_sb[(0, 1, t)] = load_por(0, 1, t)
        for t in range(PACK):
            por_sb[(1, 0, t)] = load_por(1, 0, t)
        w3_raw = [load_w3(0), load_w3(1)]
        for t in range(PACK):
            por_sb[(1, 1, t)] = load_por(1, 1, t)

        w2_codes = held([P, 2 * H], U8, "w2_codes")
        w2_sc = held([P, H], U8, "w2_sc")
        nc.vector.tensor_copy(
            w2_codes[:].rearrange("p (b t m e) -> p b t m e", b=2, t=PACK, e=2),
            w2_raw[:].rearrange("p (b m t e) -> p b t m e", b=2, t=PACK, e=2),
        )
        nc.vector.tensor_copy(
            w2_sc[:].rearrange("p (b t m) -> p b t m", b=2, t=PACK),
            w2_plane[:].rearrange("p (b m t) -> p b t m", b=2, t=PACK),
        )

        v_plane = held([P, S], U8, "v_plane")
        nc.vector.tensor_copy(v_plane[:], tab_plane[:].indirect(offsets[:]))
        v_words = []
        for a in range(2):
            words = held([P, S], U32, "v%d" % a)
            nc.vector.tensor_copy(words[:], tab_sb[a][:].bitcast(U32).indirect(offsets[:]))
            v_words.append(words)

        w1_q = {}

        def round_w1(grouped, b, a, u, on_vector):
            src = w1_raw[(b, a)][:].rearrange("p i (m u e) -> p u m i e", u=2, e=2)[:, u]
            dst = grouped.rearrange("p (e m i) -> p m i e", e=2, i=PACK)
            if on_vector:
                nc.vector.tensor_copy(dst, src)
            else:
                nc.scalar.copy(dst, src)

        def quantize(grouped, name, tag=None):
            width = grouped.shape[1] // PACK
            codes = held([P, width], U32, name + "c", tag)
            scales = held([P, width], U8, name + "s")
            nc.vector.quantize_mx(out=codes[:].bitcast(FP8X4), scales=scales[:], in_=grouped)
            return codes, scales

        w1_bf = {}

        def round_w1_pass(b, a, behind):
            w1_bf[(b, a)] = held([P, PACK * PASS], BF16, "w1bf%d%d" % (b, a), behind)
            for u in range(2):
                round_w1(w1_bf[(b, a)][:, 2 * PASS * u : 2 * PASS * (u + 1)], b, a, u, False)

        def quantize_w1_pass(b, a, behind):
            codes, scales = quantize(w1_bf[(b, a)][:], "w1q%d%d" % (b, a), behind)
            for t in range(PACK):
                w1_q[(b, a, t)] = (codes[:, P * t : P * (t + 1)], scales[:, P * t : P * (t + 1)])

        def quantize_pair(a, u):
            codes, scales = quantize(w1_bf[(0, a, u)][:], "w1q0%d%d" % (a, u))
            for e in range(2):
                w1_q[(0, a, 2 * u + e)] = (codes[:, P * e : P * (e + 1)], scales[:, P * e : P * (e + 1)])

        for a in range(2):
            for u in range(2):
                behind = {(0, 0): "tab1", (1, 0): "w1raw00"}.get((a, u))
                w1_bf[(0, a, u)] = held([P, 2 * PASS], BF16, "w1bf0%d%d" % (a, u), behind)
                round_w1(w1_bf[(0, a, u)][:], 0, a, u, u == 0)
            if a == 0:
                for u in range(2):
                    quantize_pair(0, u)

        diff = {}
        h_bf = {}
        h_q = {}
        w3_q = []

        def dye_pass(dye, a, b, t, c0, width):
            codes, scales = w1_q[(b, a, t)]
            nc.tensor.matmul_mx(
                out=dye[:],
                lhsT=codes.bitcast(FP8X4),
                lhsT_scale=scales,
                rhs=v_words[a][:, c0 : c0 + width].bitcast(FP8X4),
                rhs_scale=v_plane[4 * a : P, c0 : c0 + width],
                start=(a == 0),
                stop=(a == 1),
            )

        def open_step(b, t, c0, width):
            half, lo = divmod(c0, HALF)
            strand = strand_ps.tile([P, width], F32, name="strand")
            col = PASS * b + P * t
            nc.tensor.matmul_mx(
                out=strand[:],
                lhsT=w2_codes[:, 2 * col : 2 * (col + P)].bitcast(FP4X4),
                lhsT_scale=w2_sc[:, col : col + P],
                rhs=xs_sb[half][:, lo : lo + width].bitcast(FP8X4),
                rhs_scale=xs_plane[:, c0 : c0 + width],
                start=True,
                stop=True,
            )
            dye = dye_ps.tile([P, width], F32, name="dye")
            dye_pass(dye, 0, b, t, c0, width)
            return strand, dye

        def weigh(strand, dye, b, t, c0, width):
            half, lo = divmod(c0, HALF)
            dye_pass(dye, 1, b, t, c0, width)
            weighted = ring.tile([P, width], F32, name="weighted")
            nc.vector.tensor_tensor(weighted[:], dye[:], por_sb[(b, half, t)][:, lo : lo + width], MULT)
            return strand, weighted

        def difference(b, t, c0, width, strand, weighted):
            if t == 0:
                diff[(b, c0)] = held([P, PACK, width], F32, "diff%d_%d" % (b, c0))
            nc.vector.scalar_tensor_tensor(
                diff[(b, c0)][:, t, :], strand[:], gains[:, b, t : t + 1], weighted[:], MULT, SUB
            )

        def magnitude(b, c0, lo, width, behind=None):
            grouped = held([P, width * PACK], BF16, "hbf%d_%d" % (b, c0 + lo), behind)
            piece = min(width, PIECE)
            for at in range(0, width, piece):
                nc.scalar.activation(
                    grouped[:, PACK * at : PACK * (at + piece)].rearrange("p (c e t) -> p c t e", e=4, t=PACK),
                    diff[(b, c0)][:, :, lo + at : lo + at + piece].rearrange("p t (c e) -> p c t e", e=4),
                    ABS,
                )
            h_bf[(b, c0 + lo)] = grouped

        def quantize_h(b, c0, behind=None):
            codes, scales = quantize(h_bf[(b, c0)][:], "hq%d_%d" % (b, c0), behind)
            for lo in range(0, codes[:].shape[1], P):
                h_q[(b, c0 + lo)] = (codes, scales, lo)

        def scores(c0, piece):
            acc = out_ps.tile([P, 2, piece], F32, name="acc")
            for nt in range(2):
                for b in range(2):
                    codes, scales, at = h_q[(b, c0)]
                    nc.tensor.matmul_mx(
                        out=acc[:, nt, :],
                        lhsT=w3_q[0][:, N * b + P * nt : N * b + P * (nt + 1)].bitcast(FP8X4),
                        lhsT_scale=w3_q[1][:, N * b + P * nt : N * b + P * (nt + 1)],
                        rhs=codes[:, at : at + piece].bitcast(FP8X4),
                        rhs_scale=scales[:, at : at + piece],
                        start=(b == 0),
                        stop=(b == 1),
                    )
            staged = held([P, 2, piece], F32, "staged%d" % c0)
            nc.scalar.copy(staged[:], acc[:])
            nc.sync.dma_start(out.rearrange("(c p) j -> p c j", p=P)[:, :, c0 : c0 + piece], staged[:])

        w3_bf = []

        def round_w3(behind):
            grouped = held([P, 2 * N * PACK], BF16, "w3bf", behind)
            for b in range(2):
                nc.scalar.copy(
                    grouped[:, N * PACK * b : N * PACK * (b + 1)].rearrange("p (c e t) -> p c t e", e=4, t=PACK),
                    w3_raw[b][:].rearrange("p t (c e) -> p c t e", e=4),
                )
            w3_bf.append(grouped)

        groups = [(0, 0, 512), (0, 512, 512), (1, 0, 512), (1, 512, 256), (1, 768, 128), (1, 896, 128)]
        steps = [(b, t, c0, width) for (b, c0, width) in groups for t in range(PACK)]
        opened = [open_step(*step) for step in steps[:3]]
        before = None
        for n, step in enumerate(steps + [None]):
            if step is not None:
                if n >= 3:
                    opened.append(open_step(*step))
                if n in (0, 2):
                    quantize_pair(1, n // 2)
                made = weigh(*opened[n], *step)
            if before is not None:
                difference(*before)
            if n == 2:
                round_w1_pass(1, 0, "por002")
            if n == 4:
                magnitude(0, 0, 0, PIECE)
            if n == 5:
                round_w1_pass(1, 1, "por011")
                magnitude(0, 0, PIECE, PIECE, "w1raw11")
            if n == 6:
                quantize_w1_pass(1, 0, "por012")
            if n == 7:
                quantize_w1_pass(1, 1, None)
            if n == 8:
                magnitude(0, HALF, 0, HALF)
            if n == 9:
                quantize_h(0, 0, "por100")
                quantize_h(0, PIECE, "por101")
            if n == 10:
                round_w3("por102")
            if n == 11:
                quantize_h(0, HALF, "por103")
            if n == 12:
                magnitude(1, 0, 0, HALF)
            if n == 13:
                w3_q.extend(quantize(w3_bf[0][:], "w3q", "diff0_512"))
            if n == 15:
                quantize_h(1, 0)
                scores(0, PIECE)
                scores(PIECE, PIECE)
            if n in (16, 20, 24):
                magnitude(1, before[2], 0, before[3])
            if n in (18, 22, 24):
                b, c0, width = groups[{18: 3, 22: 4, 24: 5}[n]]
                quantize_h(b, c0)
                scores(c0, width)
            before = step + made if step is not None else None
